import numpy as np
import ml_dtypes


def mxq(x, axis, fmt="e4m3"):
    dtype, down = {"e4m3": (ml_dtypes.float8_e4m3fn, 7), "e5m2": (ml_dtypes.float8_e5m2, 14)}[fmt]
    v = np.moveaxis(np.asarray(x, np.float32).astype(ml_dtypes.bfloat16).astype(np.float64), axis, -1)
    blocks = v.reshape(v.shape[:-1] + (-1, 32))
    amax = np.abs(blocks).max(-1, keepdims=True)
    byte = np.maximum(np.where(amax > 0, np.frexp(amax)[1] - 1 + 127, 0) - down, 1)
    scale = np.exp2(byte - 127.0)
    codes = (blocks / scale).astype(np.float32).astype(dtype).astype(np.float64)
    return np.moveaxis((codes * scale).reshape(v.shape), -1, axis)


WIDE = False


def mx_kscale(k):
    if not WIDE:
        return np.ones(k)
    levels = np.array([10, -10, 5, -5, 0])
    if k % 512:
        return np.exp2(np.random.permutation(np.resize(levels, k // 32))).repeat(32)
    a = np.empty((k // 512, 16))
    for p in range(k // 512):
        a[p, :8] = np.random.permutation(np.resize(levels, 8))
        for g in range(8):
            far = levels[np.abs(levels - a[p, g]) >= 10]
            a[p, g + 8] = far[np.random.randint(len(far))]
    return np.exp2(a.ravel()).repeat(32)


def f64(x):
    return np.asarray(x).astype(np.float64)


def striped(idx):
    return np.tile(idx.reshape(-1, 16).T, (8, 1)).astype(np.uint16)


def unstriped(offs):
    return offs[:16].T.reshape(-1).astype(np.int64)


E2M1 = np.array([0.0, 0.5, 1.0, 1.5, 2.0, 3.0, 4.0, 6.0, -0.0, -0.5, -1.0, -1.5, -2.0, -3.0, -4.0, -6.0])


def pack_weight(w, fmt):
    k, n = w.shape
    w = f64(np.asarray(w, np.float32).astype(ml_dtypes.bfloat16)).reshape(k // 32, 32, n)
    amax = np.abs(w).max(1)
    if fmt == "e4m3":
        byte = np.frexp(amax)[1] - 1 + 127 - 7
    else:
        mant, ex = np.frexp(amax / 6.0)
        byte = np.where(mant > 0.5, ex, ex - 1) + 127
    byte = np.clip(np.where(amax > 0, byte, 1), 1, 254)
    scaled = (w * np.exp2(127.0 - byte)[:, None, :]).reshape(k, n).astype(np.float32)
    by_word = np.ascontiguousarray(scaled.reshape(k // 512, 128, 4, n).transpose(0, 1, 3, 2))
    if fmt == "e4m3":
        words = by_word.astype(ml_dtypes.float8_e4m3fn).view(np.uint8)
    else:
        c = by_word.astype(ml_dtypes.float4_e2m1fn).view(np.uint8) & 0xF
        words = (c[..., 0::2] | (c[..., 1::2] << 4)).reshape(k // 512, 128, 2 * n)
    return np.ascontiguousarray(words), np.ascontiguousarray(byte.astype(np.uint8).reshape(k // 512, 16, n))


def unpack_weight(words, scales, fmt):
    g, _, n = scales.shape
    words = np.ascontiguousarray(words).reshape(g, 128, n, -1)
    if fmt == "e4m3":
        vals = words.view(ml_dtypes.float8_e4m3fn).astype(np.float64)
    else:
        nib = np.empty((g, 128, n, 4), np.uint8)
        nib[..., 0::2] = words & 0xF
        nib[..., 1::2] = words >> 4
        vals = E2M1[nib]
    vals = vals * np.repeat(np.exp2(scales.astype(np.float64) - 127.0), 8, axis=1)[..., None]
    return vals.transpose(0, 1, 3, 2).reshape(g * 512, n)


def gelu(v):
    return 0.5 * v * (1.0 + np.tanh(np.sqrt(2.0 / np.pi) * (v + 0.044715 * v**3)))


def bf(x):
    return np.asarray(x, np.float32).astype(ml_dtypes.bfloat16)


def planes(Y):
    n, m = Y.shape
    b = f64(bf(Y)).reshape(n // 32, 32, m)
    amax = np.abs(b).max(1)
    byte = np.clip(np.where(amax > 0, np.frexp(amax)[1] - 1 + 127 - 7, 1), 1, 254)
    codes = (b * np.exp2(127.0 - byte)[:, None, :]).reshape(n, m).astype(np.float32).astype(ml_dtypes.float8_e4m3fn).view(np.uint8)
    words = codes.reshape(n // 512, 128, 4, m).transpose(0, 1, 3, 2)
    return np.ascontiguousarray(words), np.ascontiguousarray(byte.astype(np.uint8).reshape(n // 512, 16, m))


K, H, N, T, S, T2, P = 1024, 1024, 512, 4096, 1024, 2048, 1024

def setup_inputs():
    n = np.random.standard_normal
    s = mx_kscale(K)[:, None]
    u = mx_kscale(H)[:, None]
    d = {}
    d["tab_words"], d["tab_scales"] = pack_weight(n((K, T)) * s, "e4m3")
    d["offs"] = striped(np.random.permutation(T)[:S])
    d["w1"] = (1.4 * n((K, H)) / K**0.5 / s).astype(np.float32)
    d["gain"] = (1.4 * np.exp(0.3 * n(H)) * u[:, 0]).astype(np.float32)
    d["page0"] = (n((H, T2)) * u).astype(np.float32)
    d["wgs"] = np.exp(0.3 * n((128, S))).astype(np.float32)
    d["offs2"] = striped(np.random.permutation(T2)[:S])
    d["offs3"] = striped(np.random.permutation(T2)[:P])
    d["b2"] = (0.6 * n(H) * u[:, 0]).astype(np.float32)
    d["w4_words"], d["w4_scales"] = pack_weight(n((H, N)) / H**0.5 / u, "e2m1")
    return d

def reference(tab_words, tab_scales, offs, w1, gain, page0, wgs, offs2, offs3, b2, w4_words, w4_scales):
    v = unpack_weight(tab_words, tab_scales, "e4m3")[:, unstriped(offs)]
    e = mxq(f64(w1), 0, "e4m3").T @ v
    h = np.tanh(e) * f64(gain)[:, None]
    page = f64(page0).copy()
    page[:, unstriped(offs2)] = np.tile(f64(wgs), (H // 128, 1)) * h
    x = page[:, unstriped(offs3)] + f64(b2)[:, None]
    w4 = unpack_weight(w4_words, w4_scales, "e2m1")
    y = w4.T @ mxq(x, 0, "e4m3")
    words, scales = planes(page)
    return y, page, words, scales

@@ -1,0 +1,334 @@
+from contextlib import ExitStack
+
+import concourse.mybir as mybir
+
+K, H, N, T, S, T2, J = 1024, 1024, 512, 4096, 1024, 2048, 1024
+FLOPS = 2 * K * H * S + 2 * H * N * J
+
+F32 = mybir.dt.float32
+BF16 = mybir.dt.bfloat16
+I32 = mybir.dt.int32
+U32 = mybir.dt.uint32
+U16 = mybir.dt.uint16
+U8 = mybir.dt.uint8
+FP8X4 = mybir.dt.float8_e4m3fn_x4
+FP4X4 = mybir.dt.float4_e2m1fn_x4
+ACT = mybir.ActivationFunctionType
+MULT = mybir.AluOpType.mult
+
+P = 128
+PACK = 4
+GROUP = P * PACK
+QUADS = 4
+QROWS = 32
+BANK = 512
+LIST_COLS = BANK // 16
+
+
+def tile_list_roast_profile_page_kernel(
+    tc, tab_words, tab_scales, offs, w1, gain, page0, wgs, offs2, offs3, b2, w4_words, w4_scales,
+    out_0, out_1, out_2, out_3,
+):
+    nc = tc.nc
+    with ExitStack() as ctx:
+        lists = ctx.enter_context(tc.tile_pool(name="lists", bufs=1))
+        keep = ctx.enter_context(tc.tile_pool(name="keep", bufs=1))
+        ring = ctx.enter_context(tc.tile_pool(name="ring", bufs=2))
+        psum = ctx.enter_context(tc.psum_pool(name="psum", bufs=8))
+
+        pick = lists.tile([P, S // 16], U16, name="pick")
+        put = lists.tile([P, S // 16], U16, name="put")
+        read = lists.tile([P, J // 16], U16, name="read")
+
+        slices = [(b, t) for b in range(2) for t in range(PACK)]
+        halves = [slice(h * BANK, (h + 1) * BANK) for h in range(2)]
+        list_halves = [slice(h * LIST_COLS, (h + 1) * LIST_COLS) for h in range(2)]
+
+        tab_planes = keep.tile([P, T], U8, name="tab_planes", align_bytes=64)
+        w4_planes = keep.tile([P, 2 * N], U8, name="w4_planes", align_bytes=64)
+        gain_cols = keep.tile([P, 2, PACK], F32, name="gain_cols")
+        bias_cols = keep.tile([P, 2, PACK], F32, name="bias_cols")
+        warm = keep.tile([P, 8], F32, name="warm")
+        nc.vector.memset(tab_planes[:, : T // 2].bitcast(I32), 0)
+        nc.gpsimd.memset(tab_planes[:, T // 2 :].bitcast(I32), 0)
+        nc.vector.memset(w4_planes[:].bitcast(I32), 0)
+        nc.vector.memset(warm[:], 0.0)
+        nc.scalar.activation(warm[:, 4:5], warm[:, 0:1], ACT.Tanh)
+
+        def load_table_planes():
+            for q in range(QUADS):
+                nc.sync.dma_start(
+                    out=tab_planes[QROWS * q : QROWS * q + 8, :].bitcast(I32),
+                    in_=tab_scales[:, 4 * q : 4 * q + 4, :].bitcast(I32),
+                )
+
+        def load_w4_planes():
+            for q in range(QUADS):
+                nc.sync.dma_start(
+                    out=w4_planes[QROWS * q : QROWS * q + 4, :].bitcast(I32).rearrange("r (a c) -> r a c", a=2),
+                    in_=w4_scales[:, 4 * q : 4 * q + 4, :].bitcast(I32).rearrange("a r c -> r a c"),
+                )
+
+        tab = [ring.tile([P, T], U32, name="tab%d" % a, tag="wide", align_bytes=64) for a in range(2)]
+        w1_raw = {}
+        for b in range(2):
+            for a in range(2):
+                w1_raw[a, b] = ring.tile([P, PACK, GROUP], F32, name="w1_raw%d%d" % (a, b), tag="raw%d" % b, align_bytes=64)
+        page = {bt: keep.tile([P, T2], F32, name="page%d%d" % bt) for bt in slices}
+        wgs_dealt = [keep.tile([P, S], F32, name="wgs_dealt%d" % t) for t in range(PACK)]
+        w4_codes = [keep.tile([P, 2 * N], U8, name="w4_codes%d" % a, align_bytes=64) for a in range(2)]
+
+        w1_rows = w1.rearrange("(a p j) (b c) -> a b p j c", a=2, j=PACK, b=2)
+        page_rows = page0.rearrange("(b p t) m -> b t p m", b=2, t=PACK)
+        out1_rows = out_1.rearrange("(b p t) m -> b t p m", b=2, t=PACK)
+        wgs_rows = wgs.rearrange("(q t) j -> t q j", t=PACK)
+
+        def load_table(a):
+            nc.sync.dma_start(out=tab[a][:].bitcast(I32), in_=tab_words[a].rearrange("p t i -> p (t i)").bitcast(I32))
+
+        def load_w1(a, b):
+            nc.sync.dma_start(out=w1_raw[a, b][:], in_=w1_rows[a, b])
+
+        def load_page(b, t):
+            nc.sync.dma_start(out=page[b, t][:], in_=page_rows[b, t])
+
+        def load_wgs(t):
+            for q in range(QUADS):
+                nc.sync.dma_start(out=wgs_dealt[t][QROWS * q : QROWS * (q + 1), :], in_=wgs_rows[t])
+
+        load_table_planes()
+        nc.sync.dma_start(pick[:], offs)
+        load_w1(0, 0)
+        load_table(0)
+        load_w1(1, 0)
+        nc.sync.dma_start(out=gain_cols[:], in_=gain.rearrange("(b p t) -> p b t", b=2, t=PACK))
+        nc.sync.dma_start(put[:], offs2)
+        load_table(1)
+        load_wgs(0)
+        load_page(0, 0)
+        load_wgs(1)
+        nc.sync.dma_start(read[:], offs3)
+        nc.sync.dma_start(out=bias_cols[:], in_=b2.rearrange("(b p t) -> p b t", b=2, t=PACK))
+        load_w1(0, 1)
+        load_page(0, 1)
+        load_wgs(2)
+        load_w1(1, 1)
+        load_page(0, 2)
+        load_wgs(3)
+        load_page(1, 3)
+        load_page(0, 3)
+        for t in range(PACK - 1):
+            load_page(1, t)
+        for a in range(2):
+            nc.sync.dma_start(out=w4_codes[a][:].bitcast(I32), in_=w4_words[a].bitcast(I32))
+        load_w4_planes()
+
+        w1_codes = {}
+        w1_planes = {}
+
+        def quantise_w1(a, b, copy):
+            grouped = ring.tile([P, GROUP * PACK], BF16, name="w1_grouped", tag="woven", bufs=4, align_bytes=64)
+            copy(
+                grouped[:].rearrange("p (t m j) -> p m j t", t=PACK, j=PACK),
+                w1_raw[a, b][:].rearrange("p j (m t) -> p m j t", t=PACK),
+            )
+            w1_codes[a, b] = keep.tile([P, GROUP], U32, name="w1_codes%d%d" % (a, b), align_bytes=64)
+            w1_planes[a, b] = keep.tile([P, GROUP], U8, name="w1_planes%d%d" % (a, b), align_bytes=64)
+            nc.vector.quantize_mx(out=w1_codes[a, b][:].bitcast(FP8X4), scales=w1_planes[a, b][:], in_=grouped[:])
+
+        picked_planes = keep.tile([P, S], U8, name="picked_planes", align_bytes=64)
+        picked = [keep.tile([P, S], U32, name="picked%d" % a, align_bytes=64) for a in range(2)]
+
+        quantise_w1(0, 0, nc.vector.tensor_copy)
+        nc.vector.tensor_copy(picked_planes[:], tab_planes[:].indirect(pick[:]))
+        nc.vector.tensor_copy(picked[0][:], tab[0][:].indirect(pick[:]))
+        quantise_w1(1, 0, nc.vector.tensor_copy)
+        for h in range(2):
+            nc.vector.tensor_copy(picked[1][:, halves[h]], tab[1][:].indirect(pick[:, list_halves[h]]))
+
+        factor = {}
+        feature = {}
+
+        def make_factor(b, t):
+            if b == 0:
+                factor[b, t] = ring.tile([P, S], F32, name="factor", tag="factor")
+            else:
+                factor[b, t] = wgs_dealt[t]
+            nc.scalar.activation(factor[b, t][:], wgs_dealt[t][:], ACT.Copy, scale=gain_cols[:, b, t : t + 1])
+
+        def make_feature(b, t):
+            feature[b, t] = ring.tile([P, S], F32, name="feature", tag="feature")
+            cols = slice(P * t, P * (t + 1))
+            for h in range(2):
+                acc = psum.tile([P, BANK], F32, name="acc", tag="bank")
+                for a in range(2):
+                    nc.tensor.matmul_mx(
+                        out=acc[:],
+                        lhsT=w1_codes[a, b][:, cols].bitcast(FP8X4),
+                        lhsT_scale=w1_planes[a, b][:, cols],
+                        rhs=picked[a][:, halves[h]].bitcast(FP8X4),
+                        rhs_scale=picked_planes[4 * a :, halves[h]],
+                        start=(a == 0),
+                        stop=(a == 1),
+                    )
+                nc.scalar.activation(feature[b, t][:, halves[h]], acc[:], ACT.Tanh)
+
+        def scatter(b, t):
+            if (b, t) == slices[0]:
+                for h in range(2):
+                    nc.vector.tensor_tensor(
+                        page[b, t][:].indirect(put[:, list_halves[h]]),
+                        feature[b, t][:, halves[h]], factor[b, t][:, halves[h]], MULT,
+                    )
+            else:
+                nc.vector.tensor_tensor(page[b, t][:].indirect(put[:]), feature[b, t][:], factor[b, t][:], MULT)
+            nc.sync.dma_start(out=out1_rows[b, t], in_=page[b, t][:])
+
+        page_bf = {}
+        x_bf = {}
+
+        def round_page(b, t):
+            if t == 0:
+                page_bf[b] = ring.tile([P, PACK, T2], BF16, name="page_bf", tag="wide", align_bytes=64)
+            nc.scalar.copy(page_bf[b][:, t, :], page[b, t][:])
+
+        def fetch(b, t):
+            if t == 0:
+                x_bf[b] = ring.tile([P, PACK, J], BF16, name="x_bf", tag="raw1", align_bytes=64)
+            fetched = ring.tile([P, J], F32, name="fetched", tag="raw0", align_bytes=64)
+            if (b, t) == slices[-1]:
+                for h in range(2):
+                    nc.vector.tensor_copy(fetched[:, halves[h]], page[b, t][:].indirect(read[:, list_halves[h]]))
+                    nc.scalar.activation(
+                        x_bf[b][:, t, halves[h]], fetched[:, halves[h]], ACT.Identity, bias=bias_cols[:, b, t : t + 1]
+                    )
+            else:
+                nc.vector.tensor_copy(fetched[:], page[b, t][:].indirect(read[:]))
+                nc.scalar.activation(x_bf[b][:, t, :], fetched[:], ACT.Identity, bias=bias_cols[:, b, t : t + 1])
+
+        def weave(rows, cols, copy):
+            woven = ring.tile([P, BANK * PACK], BF16, name="woven", tag="woven", bufs=4, align_bytes=64)
+            copy(
+                woven[:].rearrange("p (c i t) -> p c t i", i=4, t=PACK),
+                rows[:, :, cols].rearrange("p t (c i) -> p c t i", i=4),
+            )
+            return woven
+
+        x_codes = [keep.tile([P, J], U32, name="x_codes%d" % b, align_bytes=64) for b in range(2)]
+        x_planes = [keep.tile([P, J], U8, name="x_planes%d" % b, align_bytes=64) for b in range(2)]
+        page_codes = [keep.tile([P, T2], U32, name="page_codes%d" % b, align_bytes=64) for b in range(2)]
+        page_planes = [keep.tile([P, T2], U8, name="page_planes%d" % b, align_bytes=64) for b in range(2)]
+
+        def quantise_x(b, h, woven):
+            nc.vector.quantize_mx(
+                out=x_codes[b][:, halves[h]].bitcast(FP8X4), scales=x_planes[b][:, halves[h]], in_=woven[:]
+            )
+
+        def quantise_page(b, c, woven):
+            cols = slice(c * BANK, (c + 1) * BANK)
+            nc.vector.quantize_mx(out=page_codes[b][:, cols].bitcast(FP8X4), scales=page_planes[b][:, cols], in_=woven[:])
+            nc.sync.dma_start(
+                out=out_2[b].rearrange("p m t -> p (m t)").bitcast(I32)[:, cols],
+                in_=page_codes[b][:, cols].bitcast(I32),
+            )
+
+        def store_page_planes(b):
+            for q in range(QUADS):
+                nc.sync.dma_start(
+                    out=out_3[b, 4 * q : 4 * q + 4, :].bitcast(I32),
+                    in_=page_planes[b][QROWS * q : QROWS * q + 4, :].bitcast(I32),
+                )
+
+        score_acc = {}
+
+        def score_pass(b, h):
+            for n in range(N // P):
+                if b == 0:
+                    score_acc[n, h] = psum.tile([P, BANK], F32, name="score_acc", tag="bank")
+                nc.tensor.matmul_mx(
+                    out=score_acc[n, h][:],
+                    lhsT=w4_codes[b][:, 2 * P * n : 2 * P * (n + 1)].bitcast(FP4X4),
+                    lhsT_scale=w4_planes[:, N * b + P * n : N * b + P * (n + 1)],
+                    rhs=x_codes[b][:, halves[h]].bitcast(FP8X4),
+                    rhs_scale=x_planes[b][:, halves[h]],
+                    start=(b == 0),
+                    stop=(b == 1),
+                )
+
+        score = {}
+
+        def store_scores(h):
+            for n in range(N // P):
+                if h == 0:
+                    score[n] = ring.tile([P, J], F32, name="score", tag="factor" if n < 2 else "feature")
+                nc.scalar.copy(score[n][:, halves[h]], score_acc[n, h][:])
+                nc.sync.dma_start(out=out_0[P * n : P * (n + 1), halves[h]], in_=score[n][:, halves[h]])
+
+        page_chunks = [slice(c * BANK, (c + 1) * BANK) for c in range(T2 // BANK)]
+
+        make_factor(0, 0)
+        make_feature(0, 0)
+        make_factor(0, 1)
+        make_feature(0, 1)
+        scatter(0, 0)
+        make_feature(0, 2)
+        round_page(0, 0)
+        fetch(0, 0)
+        quantise_w1(0, 1, nc.scalar.copy)
+        scatter(0, 1)
+        make_factor(0, 2)
+        make_feature(0, 3)
+        round_page(0, 1)
+        fetch(0, 1)
+        quantise_w1(1, 1, nc.scalar.copy)
+        scatter(0, 2)
+        make_factor(0, 3)
+        make_feature(1, 0)
+        for t in range(PACK):
+            make_factor(1, t)
+        round_page(0, 2)
+        fetch(0, 2)
+        scatter(0, 3)
+        round_page(0, 3)
+        fetch(0, 3)
+        scatter(1, 0)
+        make_feature(1, 1)
+        scatter(1, 1)
+        for h in range(2):
+            quantise_x(0, h, weave(x_bf[0], halves[h], nc.scalar.copy))
+        quantise_page(0, 0, weave(page_bf[0], page_chunks[0], nc.scalar.copy))
+        fetch(1, 0)
+        make_feature(1, 2)
+        scatter(1, 2)
+        quantise_page(0, 1, weave(page_bf[0], page_chunks[1], nc.scalar.copy))
+        round_page(1, 0)
+        quantise_page(0, 2, weave(page_bf[0], page_chunks[2], nc.scalar.copy))
+        fetch(1, 1)
+        quantise_page(0, 3, weave(page_bf[0], page_chunks[3], nc.scalar.copy))
+        store_page_planes(0)
+        make_feature(1, 3)
+        for h in range(2):
+            score_pass(0, h)
+        round_page(1, 1)
+        round_page(1, 2)
+        fetch(1, 2)
+        scatter(1, 3)
+        last = slices[-1]
+        fetched = ring.tile([P, J], F32, name="fetched", tag="raw0", align_bytes=64)
+        for h in range(2):
+            nc.vector.tensor_copy(fetched[:, halves[h]], page[last][:].indirect(read[:, list_halves[h]]))
+        nc.scalar.copy(page_bf[1][:, 3, page_chunks[3]], page[last][:, page_chunks[3]])
+        for h in range(2):
+            nc.scalar.activation(x_bf[1][:, 3, halves[h]], fetched[:, halves[h]], ACT.Identity, bias=bias_cols[:, 1, 3:4])
+        nc.scalar.copy(page_bf[1][:, 3, : 3 * BANK], page[last][:, : 3 * BANK])
+        woven_x = [weave(x_bf[1], halves[h], nc.vector.tensor_copy) for h in range(2)]
+        for h in range(2):
+            quantise_x(1, h, woven_x[h])
+            score_pass(1, h)
+        woven_last = weave(page_bf[1], page_chunks[3], nc.scalar.copy)
+        store_scores(0)
+        store_scores(1)
+        for c in range(3):
+            quantise_page(1, c, weave(page_bf[1], page_chunks[c], nc.vector.tensor_copy))
+        quantise_page(1, 3, woven_last)
+        store_page_planes(1)

@@ -1,6 +1,7 @@
 from contextlib import ExitStack
 
 import concourse.mybir as mybir
+from concourse.masks import make_identity
 
 K, H, N, T, S, T2, J = 1024, 1024, 512, 4096, 1024, 2048, 1024
 FLOPS = 2 * K * H * S + 2 * H * N * J
@@ -34,7 +35,7 @@ def tile_list_roast_profile_page_kernel(
         lists = ctx.enter_context(tc.tile_pool(name="lists", bufs=1))
         keep = ctx.enter_context(tc.tile_pool(name="keep", bufs=1))
         ring = ctx.enter_context(tc.tile_pool(name="ring", bufs=2))
-        psum = ctx.enter_context(tc.psum_pool(name="psum", bufs=8))
+        psum = ctx.enter_context(tc.psum_pool(name="psum", bufs=4))
 
         pick = lists.tile([P, S // 16], U16, name="pick")
         put = lists.tile([P, S // 16], U16, name="put")
@@ -49,17 +50,16 @@ def tile_list_roast_profile_page_kernel(
         gain_cols = keep.tile([P, 2, PACK], F32, name="gain_cols")
         bias_cols = keep.tile([P, 2, PACK], F32, name="bias_cols")
         warm = keep.tile([P, 8], F32, name="warm")
-        nc.vector.memset(tab_planes[:, : T // 2].bitcast(I32), 0)
-        nc.gpsimd.memset(tab_planes[:, T // 2 :].bitcast(I32), 0)
+        nc.vector.memset(tab_planes[:].bitcast(I32), 0)
         nc.vector.memset(w4_planes[:].bitcast(I32), 0)
         nc.vector.memset(warm[:], 0.0)
         nc.scalar.activation(warm[:, 4:5], warm[:, 0:1], ACT.Tanh)
 
-        def load_table_planes():
+        def load_table_planes(a):
             for q in range(QUADS):
                 nc.sync.dma_start(
-                    out=tab_planes[QROWS * q : QROWS * q + 8, :].bitcast(I32),
-                    in_=tab_scales[:, 4 * q : 4 * q + 4, :].bitcast(I32),
+                    out=tab_planes[QROWS * q + 4 * a : QROWS * q + 4 * a + 4, :].bitcast(I32),
+                    in_=tab_scales[a, 4 * q : 4 * q + 4, :].bitcast(I32),
                 )
 
         def load_w4_planes():
@@ -70,18 +70,20 @@ def tile_list_roast_profile_page_kernel(
                 )
 
         tab = [ring.tile([P, T], U32, name="tab%d" % a, tag="wide", align_bytes=64) for a in range(2)]
+        wgs_rows = ring.tile([P, S], F32, name="wgs_rows", tag="woven", bufs=4, align_bytes=64)
+        spread = [
+            ring.tile([P, 4, PACK, P], F32, name="spread%d" % h, tag="raw%d1" % h, bufs=1, align_bytes=64) for h in range(2)
+        ]
         w1_raw = {}
         for b in range(2):
             for a in range(2):
-                w1_raw[a, b] = ring.tile([P, PACK, GROUP], F32, name="w1_raw%d%d" % (a, b), tag="raw%d" % b, align_bytes=64)
+                w1_raw[a, b] = ring.tile([P, PACK, GROUP], F32, name="w1_raw%d%d" % (a, b), tag="raw%d%d" % (a, b), bufs=1, align_bytes=64)
         page = {bt: keep.tile([P, T2], F32, name="page%d%d" % bt) for bt in slices}
-        wgs_dealt = [keep.tile([P, S], F32, name="wgs_dealt%d" % t) for t in range(PACK)]
         w4_codes = [keep.tile([P, 2 * N], U8, name="w4_codes%d" % a, align_bytes=64) for a in range(2)]
 
         w1_rows = w1.rearrange("(a p j) (b c) -> a b p j c", a=2, j=PACK, b=2)
         page_rows = page0.rearrange("(b p t) m -> b t p m", b=2, t=PACK)
         out1_rows = out_1.rearrange("(b p t) m -> b t p m", b=2, t=PACK)
-        wgs_rows = wgs.rearrange("(q t) j -> t q j", t=PACK)
 
         def load_table(a):
             nc.sync.dma_start(out=tab[a][:].bitcast(I32), in_=tab_words[a].rearrange("p t i -> p (t i)").bitcast(I32))
@@ -92,33 +94,48 @@ def tile_list_roast_profile_page_kernel(
         def load_page(b, t):
             nc.sync.dma_start(out=page[b, t][:], in_=page_rows[b, t])
 
-        def load_wgs(t):
-            for q in range(QUADS):
-                nc.sync.dma_start(out=wgs_dealt[t][QROWS * q : QROWS * (q + 1), :], in_=wgs_rows[t])
-
-        load_table_planes()
+        nc.sync.dma_start(out=wgs_rows[:], in_=wgs)
         nc.sync.dma_start(pick[:], offs)
+        nc.sync.dma_start(out=gain_cols[:], in_=gain.rearrange("(b p t) -> p b t", b=2, t=PACK))
         load_w1(0, 0)
         load_table(0)
+        load_table_planes(0)
         load_w1(1, 0)
-        nc.sync.dma_start(out=gain_cols[:], in_=gain.rearrange("(b p t) -> p b t", b=2, t=PACK))
-        nc.sync.dma_start(put[:], offs2)
+        load_table_planes(1)
         load_table(1)
-        load_wgs(0)
+        nc.sync.dma_start(put[:], offs2)
         load_page(0, 0)
-        load_wgs(1)
-        nc.sync.dma_start(read[:], offs3)
-        nc.sync.dma_start(out=bias_cols[:], in_=b2.rearrange("(b p t) -> p b t", b=2, t=PACK))
+
+        ident = keep.tile([P, P], F32, name="ident")
+        make_identity(nc, ident[:])
+        for h in range(2):
+            turned = psum.tile([P, 4, P], F32, name="turned", tag="bank0")
+            for c in range(4):
+                j0 = BANK * h + P * c
+                nc.tensor.transpose(turned[:, c, :], wgs_rows[:, j0 : j0 + P], ident[:])
+            nc.scalar.copy(
+                spread[h][:].rearrange("j c t (g q) -> j c t g q", g=QUADS),
+                turned[:].rearrange("j c (q t) -> j c t q", t=PACK).unsqueeze(3).to_broadcast([P, 4, PACK, QUADS, QROWS]),
+            )
+        factor = {bt: keep.tile([P, S], F32, name="factor", tag="factor%d%d" % bt, align_bytes=64) for bt in slices}
+        for t in range(PACK):
+            for h in range(2):
+                dealt = psum.tile([P, 4, P], F32, name="dealt", tag="bank0")
+                for c in range(4):
+                    nc.tensor.transpose(dealt[:, c, :], spread[h][:, c, t, :], ident[:])
+                for b in range(2):
+                    nc.scalar.activation(
+                        factor[b, t][:, halves[h]], dealt[:].rearrange("p c j -> p (c j)"), ACT.Copy,
+                        scale=gain_cols[:, b, t : t + 1],
+                    )
+
         load_w1(0, 1)
         load_page(0, 1)
-        load_wgs(2)
+        nc.sync.dma_start(read[:], offs3)
+        nc.sync.dma_start(out=bias_cols[:], in_=b2.rearrange("(b p t) -> p b t", b=2, t=PACK))
         load_w1(1, 1)
-        load_page(0, 2)
-        load_wgs(3)
-        load_page(1, 3)
-        load_page(0, 3)
-        for t in range(PACK - 1):
-            load_page(1, t)
+        for bt in slices[2:]:
+            load_page(*bt)
         for a in range(2):
             nc.sync.dma_start(out=w4_codes[a][:].bitcast(I32), in_=w4_words[a].bitcast(I32))
         load_w4_planes()
@@ -132,7 +149,9 @@ def tile_list_roast_profile_page_kernel(
                 grouped[:].rearrange("p (t m j) -> p m j t", t=PACK, j=PACK),
                 w1_raw[a, b][:].rearrange("p j (m t) -> p m j t", t=PACK),
             )
-            w1_codes[a, b] = keep.tile([P, GROUP], U32, name="w1_codes%d%d" % (a, b), align_bytes=64)
+            w1_codes[a, b] = keep.tile(
+                [P, GROUP], U32, name="w1_codes", tag="factor0%d" % (a + 1) if b else "w1_codes%d" % a, align_bytes=64
+            )
             w1_planes[a, b] = keep.tile([P, GROUP], U8, name="w1_planes%d%d" % (a, b), align_bytes=64)
             nc.vector.quantize_mx(out=w1_codes[a, b][:].bitcast(FP8X4), scales=w1_planes[a, b][:], in_=grouped[:])
 
@@ -140,27 +159,19 @@ def tile_list_roast_profile_page_kernel(
         picked = [keep.tile([P, S], U32, name="picked%d" % a, align_bytes=64) for a in range(2)]
 
         quantise_w1(0, 0, nc.vector.tensor_copy)
-        nc.vector.tensor_copy(picked_planes[:], tab_planes[:].indirect(pick[:]))
         nc.vector.tensor_copy(picked[0][:], tab[0][:].indirect(pick[:]))
         quantise_w1(1, 0, nc.vector.tensor_copy)
+        nc.vector.tensor_copy(picked_planes[:], tab_planes[:].indirect(pick[:]))
         for h in range(2):
             nc.vector.tensor_copy(picked[1][:, halves[h]], tab[1][:].indirect(pick[:, list_halves[h]]))
 
-        factor = {}
         feature = {}
-
-        def make_factor(b, t):
-            if b == 0:
-                factor[b, t] = ring.tile([P, S], F32, name="factor", tag="factor")
-            else:
-                factor[b, t] = wgs_dealt[t]
-            nc.scalar.activation(factor[b, t][:], wgs_dealt[t][:], ACT.Copy, scale=gain_cols[:, b, t : t + 1])
 
         def make_feature(b, t):
             feature[b, t] = ring.tile([P, S], F32, name="feature", tag="feature")
             cols = slice(P * t, P * (t + 1))
             for h in range(2):
-                acc = psum.tile([P, BANK], F32, name="acc", tag="bank")
+                acc = psum.tile([P, BANK], F32, name="acc", tag="bank1")
                 for a in range(2):
                     nc.tensor.matmul_mx(
                         out=acc[:],
@@ -187,24 +198,20 @@ def tile_list_roast_profile_page_kernel(
         page_bf = {}
         x_bf = {}
 
-        def round_page(b, t):
+        def round_page(b, t, cols=slice(0, T2)):
             if t == 0:
                 page_bf[b] = ring.tile([P, PACK, T2], BF16, name="page_bf", tag="wide", align_bytes=64)
-            nc.scalar.copy(page_bf[b][:, t, :], page[b, t][:])
+            nc.scalar.copy(page_bf[b][:, t, cols], page[b, t][:, cols])
 
-        def fetch(b, t):
+        def fetch(b, t, parts=1):
             if t == 0:
-                x_bf[b] = ring.tile([P, PACK, J], BF16, name="x_bf", tag="raw1", align_bytes=64)
-            fetched = ring.tile([P, J], F32, name="fetched", tag="raw0", align_bytes=64)
-            if (b, t) == slices[-1]:
-                for h in range(2):
-                    nc.vector.tensor_copy(fetched[:, halves[h]], page[b, t][:].indirect(read[:, list_halves[h]]))
-                    nc.scalar.activation(
-                        x_bf[b][:, t, halves[h]], fetched[:, halves[h]], ACT.Identity, bias=bias_cols[:, b, t : t + 1]
-                    )
-            else:
-                nc.vector.tensor_copy(fetched[:], page[b, t][:].indirect(read[:]))
-                nc.scalar.activation(x_bf[b][:, t, :], fetched[:], ACT.Identity, bias=bias_cols[:, b, t : t + 1])
+                x_bf[b] = ring.tile([P, J, PACK], BF16, name="x_bf", tag="raw%d1" % b, bufs=1, align_bytes=64)
+            fetched = ring.tile([P, J], F32, name="fetched", tag="raw%d0" % (t % 2), bufs=1, align_bytes=64)
+            for part in range(parts):
+                cols = slice(part * J // parts, (part + 1) * J // parts)
+                entries = slice(cols.start // 16, cols.stop // 16)
+                nc.vector.tensor_copy(fetched[:, cols], page[b, t][:].indirect(read[:, entries]))
+                nc.scalar.activation(x_bf[b][:, cols, t], fetched[:, cols], ACT.Identity, bias=bias_cols[:, b, t : t + 1])
 
         def weave(rows, cols, copy):
             woven = ring.tile([P, BANK * PACK], BF16, name="woven", tag="woven", bufs=4, align_bytes=64)
@@ -219,14 +226,19 @@ def tile_list_roast_profile_page_kernel(
         page_codes = [keep.tile([P, T2], U32, name="page_codes%d" % b, align_bytes=64) for b in range(2)]
         page_planes = [keep.tile([P, T2], U8, name="page_planes%d" % b, align_bytes=64) for b in range(2)]
 
-        def quantise_x(b, h, woven):
+        def quantise_x(b, h):
             nc.vector.quantize_mx(
-                out=x_codes[b][:, halves[h]].bitcast(FP8X4), scales=x_planes[b][:, halves[h]], in_=woven[:]
+                out=x_codes[b][:, halves[h]].bitcast(FP8X4),
+                scales=x_planes[b][:, halves[h]],
+                in_=x_bf[b][:, halves[h], :].rearrange("p j t -> p (j t)"),
             )
 
         def quantise_page(b, c, woven):
             cols = slice(c * BANK, (c + 1) * BANK)
             nc.vector.quantize_mx(out=page_codes[b][:, cols].bitcast(FP8X4), scales=page_planes[b][:, cols], in_=woven[:])
+
+        def store_page_codes(b, c):
+            cols = slice(c * BANK, (c + 1) * BANK)
             nc.sync.dma_start(
                 out=out_2[b].rearrange("p m t -> p (m t)").bitcast(I32)[:, cols],
                 in_=page_codes[b][:, cols].bitcast(I32),
@@ -244,7 +256,7 @@ def tile_list_roast_profile_page_kernel(
         def score_pass(b, h):
             for n in range(N // P):
                 if b == 0:
-                    score_acc[n, h] = psum.tile([P, BANK], F32, name="score_acc", tag="bank")
+                    score_acc[n, h] = psum.tile([P, BANK], F32, name="score_acc", tag="bank%d" % h)
                 nc.tensor.matmul_mx(
                     out=score_acc[n, h][:],
                     lhsT=w4_codes[b][:, 2 * P * n : 2 * P * (n + 1)].bitcast(FP4X4),
@@ -257,54 +269,54 @@ def tile_list_roast_profile_page_kernel(
 
         score = {}
 
-        def store_scores(h):
+        def empty_scores(h):
             for n in range(N // P):
                 if h == 0:
-                    score[n] = ring.tile([P, J], F32, name="score", tag="factor" if n < 2 else "feature")
+                    score[n] = keep.tile([P, J], F32, name="score", tag="factor1%d" % n, align_bytes=64)
                 nc.scalar.copy(score[n][:, halves[h]], score_acc[n, h][:])
-                nc.sync.dma_start(out=out_0[P * n : P * (n + 1), halves[h]], in_=score[n][:, halves[h]])
+
+        def store_scores(n, h):
+            nc.sync.dma_start(out=out_0[P * n : P * (n + 1), halves[h]], in_=score[n][:, halves[h]])
 
         page_chunks = [slice(c * BANK, (c + 1) * BANK) for c in range(T2 // BANK)]
 
-        make_factor(0, 0)
         make_feature(0, 0)
-        make_factor(0, 1)
         make_feature(0, 1)
         scatter(0, 0)
         make_feature(0, 2)
+        scatter(0, 1)
+        quantise_w1(0, 1, nc.scalar.copy)
         round_page(0, 0)
         fetch(0, 0)
-        quantise_w1(0, 1, nc.scalar.copy)
-        scatter(0, 1)
-        make_factor(0, 2)
         make_feature(0, 3)
+        scatter(0, 2)
+        quantise_w1(1, 1, nc.scalar.copy)
         round_page(0, 1)
         fetch(0, 1)
-        quantise_w1(1, 1, nc.scalar.copy)
-        scatter(0, 2)
-        make_factor(0, 3)
         make_feature(1, 0)
-        for t in range(PACK):
-            make_factor(1, t)
+        scatter(0, 3)
         round_page(0, 2)
         fetch(0, 2)
-        scatter(0, 3)
         round_page(0, 3)
         fetch(0, 3)
+        def finish_page_chunk(c):
+            quantise_page(0, c, weave(page_bf[0], page_chunks[c], nc.scalar.copy))
+            store_page_codes(0, c)
+
         scatter(1, 0)
         make_feature(1, 1)
         scatter(1, 1)
         for h in range(2):
-            quantise_x(0, h, weave(x_bf[0], halves[h], nc.scalar.copy))
-        quantise_page(0, 0, weave(page_bf[0], page_chunks[0], nc.scalar.copy))
+            quantise_x(0, h)
+        finish_page_chunk(0)
+        finish_page_chunk(1)
         fetch(1, 0)
         make_feature(1, 2)
         scatter(1, 2)
-        quantise_page(0, 1, weave(page_bf[0], page_chunks[1], nc.scalar.copy))
+        finish_page_chunk(2)
         round_page(1, 0)
-        quantise_page(0, 2, weave(page_bf[0], page_chunks[2], nc.scalar.copy))
         fetch(1, 1)
-        quantise_page(0, 3, weave(page_bf[0], page_chunks[3], nc.scalar.copy))
+        finish_page_chunk(3)
         store_page_planes(0)
         make_feature(1, 3)
         for h in range(2):
@@ -313,22 +325,19 @@ def tile_list_roast_profile_page_kernel(
         round_page(1, 2)
         fetch(1, 2)
         scatter(1, 3)
-        last = slices[-1]
-        fetched = ring.tile([P, J], F32, name="fetched", tag="raw0", align_bytes=64)
+        round_page(1, 3, slice(0, T2 // 2))
+        fetch(1, 3, parts=2)
+        round_page(1, 3, slice(T2 // 2, T2))
         for h in range(2):
-            nc.vector.tensor_copy(fetched[:, halves[h]], page[last][:].indirect(read[:, list_halves[h]]))
-        nc.scalar.copy(page_bf[1][:, 3, page_chunks[3]], page[last][:, page_chunks[3]])
-        for h in range(2):
-            nc.scalar.activation(x_bf[1][:, 3, halves[h]], fetched[:, halves[h]], ACT.Identity, bias=bias_cols[:, 1, 3:4])
-        nc.scalar.copy(page_bf[1][:, 3, : 3 * BANK], page[last][:, : 3 * BANK])
-        woven_x = [weave(x_bf[1], halves[h], nc.vector.tensor_copy) for h in range(2)]
-        for h in range(2):
-            quantise_x(1, h, woven_x[h])
+            quantise_x(1, h)
             score_pass(1, h)
-        woven_last = weave(page_bf[1], page_chunks[3], nc.scalar.copy)
-        store_scores(0)
-        store_scores(1)
-        for c in range(3):
+        for h in range(2):
+            empty_scores(h)
+        for c in range(4):
             quantise_page(1, c, weave(page_bf[1], page_chunks[c], nc.vector.tensor_copy))
-        quantise_page(1, 3, woven_last)
+        for c in range(4):
+            store_page_codes(1, c)
+            if c < 3:
+                for k in range(3 * c, min(3 * c + 3, 8)):
+                    store_scores(k % 4, k // 4)
         store_page_planes(1)

@@ -45,7 +45,7 @@ def tile_list_roast_profile_page_kernel(
         halves = [slice(h * BANK, (h + 1) * BANK) for h in range(2)]
         list_halves = [slice(h * LIST_COLS, (h + 1) * LIST_COLS) for h in range(2)]
 
-        tab_planes = keep.tile([P, T], U8, name="tab_planes", align_bytes=64)
+        tab_planes = keep.tile([P, T], U8, name="tab_planes", tag="tab_planes", align_bytes=64)
         w4_planes = keep.tile([P, 2 * N], U8, name="w4_planes", align_bytes=64)
         gain_cols = keep.tile([P, 2, PACK], F32, name="gain_cols")
         bias_cols = keep.tile([P, 2, PACK], F32, name="bias_cols")
@@ -55,12 +55,11 @@ def tile_list_roast_profile_page_kernel(
         nc.vector.memset(warm[:], 0.0)
         nc.scalar.activation(warm[:, 4:5], warm[:, 0:1], ACT.Tanh)
 
-        def load_table_planes(a):
-            for q in range(QUADS):
-                nc.sync.dma_start(
-                    out=tab_planes[QROWS * q + 4 * a : QROWS * q + 4 * a + 4, :].bitcast(I32),
-                    in_=tab_scales[a, 4 * q : 4 * q + 4, :].bitcast(I32),
-                )
+        for q in range(QUADS):
+            nc.gpsimd.dma_start(
+                out=tab_planes[QROWS * q : QROWS * q + 8, :].bitcast(I32),
+                in_=tab_scales[:, 4 * q : 4 * q + 4, :].bitcast(I32),
+            )
 
         def load_w4_planes():
             for q in range(QUADS):
@@ -99,9 +98,7 @@ def tile_list_roast_profile_page_kernel(
         nc.sync.dma_start(out=gain_cols[:], in_=gain.rearrange("(b p t) -> p b t", b=2, t=PACK))
         load_w1(0, 0)
         load_table(0)
-        load_table_planes(0)
         load_w1(1, 0)
-        load_table_planes(1)
         load_table(1)
         nc.sync.dma_start(put[:], offs2)
         load_page(0, 0)
@@ -113,7 +110,7 @@ def tile_list_roast_profile_page_kernel(
             for c in range(4):
                 j0 = BANK * h + P * c
                 nc.tensor.transpose(turned[:, c, :], wgs_rows[:, j0 : j0 + P], ident[:])
-            nc.scalar.copy(
+            (nc.scalar.copy, nc.vector.tensor_copy)[h](
                 spread[h][:].rearrange("j c t (g q) -> j c t g q", g=QUADS),
                 turned[:].rearrange("j c (q t) -> j c t q", t=PACK).unsqueeze(3).to_broadcast([P, 4, PACK, QUADS, QROWS]),
             )
@@ -144,7 +141,10 @@ def tile_list_roast_profile_page_kernel(
         w1_planes = {}
 
         def quantise_w1(a, b, copy):
-            grouped = ring.tile([P, GROUP * PACK], BF16, name="w1_grouped", tag="woven", bufs=4, align_bytes=64)
+            if (a, b) == (1, 0):
+                grouped = keep.tile([P, GROUP * PACK], BF16, name="w1_grouped", tag="picked_planes", align_bytes=64)
+            else:
+                grouped = ring.tile([P, GROUP * PACK], BF16, name="w1_grouped", tag="woven", bufs=4, align_bytes=64)
             copy(
                 grouped[:].rearrange("p (t m j) -> p m j t", t=PACK, j=PACK),
                 w1_raw[a, b][:].rearrange("p j (m t) -> p m j t", t=PACK),
@@ -155,12 +155,12 @@ def tile_list_roast_profile_page_kernel(
             w1_planes[a, b] = keep.tile([P, GROUP], U8, name="w1_planes%d%d" % (a, b), align_bytes=64)
             nc.vector.quantize_mx(out=w1_codes[a, b][:].bitcast(FP8X4), scales=w1_planes[a, b][:], in_=grouped[:])
 
-        picked_planes = keep.tile([P, S], U8, name="picked_planes", align_bytes=64)
         picked = [keep.tile([P, S], U32, name="picked%d" % a, align_bytes=64) for a in range(2)]
 
         quantise_w1(0, 0, nc.vector.tensor_copy)
         nc.vector.tensor_copy(picked[0][:], tab[0][:].indirect(pick[:]))
         quantise_w1(1, 0, nc.vector.tensor_copy)
+        picked_planes = keep.tile([P, S], U8, name="picked_planes", tag="picked_planes", align_bytes=64)
         nc.vector.tensor_copy(picked_planes[:], tab_planes[:].indirect(pick[:]))
         for h in range(2):
             nc.vector.tensor_copy(picked[1][:, halves[h]], tab[1][:].indirect(pick[:, list_halves[h]]))
@@ -193,35 +193,37 @@ def tile_list_roast_profile_page_kernel(
                     )
             else:
                 nc.vector.tensor_tensor(page[b, t][:].indirect(put[:]), feature[b, t][:], factor[b, t][:], MULT)
+
+        def store_page(b, t):
             nc.sync.dma_start(out=out1_rows[b, t], in_=page[b, t][:])
 
-        page_bf = {}
+        page_halves = [slice(h * T2 // 2, (h + 1) * T2 // 2) for h in range(2)]
         x_bf = {}
-
-        def round_page(b, t, cols=slice(0, T2)):
-            if t == 0:
-                page_bf[b] = ring.tile([P, PACK, T2], BF16, name="page_bf", tag="wide", align_bytes=64)
-            nc.scalar.copy(page_bf[b][:, t, cols], page[b, t][:, cols])
+        x_rows = {}
 
         def fetch(b, t, parts=1):
-            if t == 0:
-                x_bf[b] = ring.tile([P, J, PACK], BF16, name="x_bf", tag="raw%d1" % b, bufs=1, align_bytes=64)
             fetched = ring.tile([P, J], F32, name="fetched", tag="raw%d0" % (t % 2), bufs=1, align_bytes=64)
             for part in range(parts):
                 cols = slice(part * J // parts, (part + 1) * J // parts)
                 entries = slice(cols.start // 16, cols.stop // 16)
                 nc.vector.tensor_copy(fetched[:, cols], page[b, t][:].indirect(read[:, entries]))
-                nc.scalar.activation(x_bf[b][:, cols, t], fetched[:, cols], ACT.Identity, bias=bias_cols[:, b, t : t + 1])
+            bias = bias_cols[:, b, t : t + 1]
+            if t == 0:
+                x_rows[b] = keep.tile([P, PACK - 1, J], BF16, name="x_rows", tag="factor00", align_bytes=64)
+            if t < PACK - 1:
+                nc.scalar.activation(x_rows[b][:, t, :], fetched[:], ACT.Identity, bias=bias)
+            for h in range(2):
+                if t == PACK - 2:
+                    weave_into(x_bf[b, h][:, :, : PACK - 1], x_rows[b][:, :, halves[h]], nc.scalar.copy)
+                if t == PACK - 1:
+                    nc.scalar.activation(x_bf[b, h][:, :, t], fetched[:, halves[h]], ACT.Identity, bias=bias)
 
-        def weave(rows, cols, copy):
-            woven = ring.tile([P, BANK * PACK], BF16, name="woven", tag="woven", bufs=4, align_bytes=64)
-            copy(
-                woven[:].rearrange("p (c i t) -> p c t i", i=4, t=PACK),
-                rows[:, :, cols].rearrange("p t (c i) -> p c t i", i=4),
-            )
-            return woven
+        def weave_into(woven, rows, copy):
+            copy(woven.rearrange("p (c i) t -> p c t i", i=4), rows.rearrange("p t (c i) -> p c t i", i=4))
 
-        x_codes = [keep.tile([P, J], U32, name="x_codes%d" % b, align_bytes=64) for b in range(2)]
+        x_codes = [
+            keep.tile([P, J], U32, name="x_codes", tag=tag, align_bytes=64) for tag in ("x_codes", "tab_planes")
+        ]
         x_planes = [keep.tile([P, J], U8, name="x_planes%d" % b, align_bytes=64) for b in range(2)]
         page_codes = [keep.tile([P, T2], U32, name="page_codes%d" % b, align_bytes=64) for b in range(2)]
         page_planes = [keep.tile([P, T2], U8, name="page_planes%d" % b, align_bytes=64) for b in range(2)]
@@ -230,12 +232,12 @@ def tile_list_roast_profile_page_kernel(
             nc.vector.quantize_mx(
                 out=x_codes[b][:, halves[h]].bitcast(FP8X4),
                 scales=x_planes[b][:, halves[h]],
-                in_=x_bf[b][:, halves[h], :].rearrange("p j t -> p (j t)"),
+                in_=x_bf[b, h].rearrange("p j t -> p (j t)"),
             )
 
         def quantise_page(b, c, woven):
             cols = slice(c * BANK, (c + 1) * BANK)
-            nc.vector.quantize_mx(out=page_codes[b][:, cols].bitcast(FP8X4), scales=page_planes[b][:, cols], in_=woven[:])
+            nc.vector.quantize_mx(out=page_codes[b][:, cols].bitcast(FP8X4), scales=page_planes[b][:, cols], in_=woven.rearrange("p m t -> p (m t)"))
 
         def store_page_codes(b, c):
             cols = slice(c * BANK, (c + 1) * BANK)
@@ -245,10 +247,10 @@ def tile_list_roast_profile_page_kernel(
             )
 
         def store_page_planes(b):
-            for q in range(QUADS):
+            for r in range(4):
                 nc.sync.dma_start(
-                    out=out_3[b, 4 * q : 4 * q + 4, :].bitcast(I32),
-                    in_=page_planes[b][QROWS * q : QROWS * q + 4, :].bitcast(I32),
+                    out=out_3[b].rearrange("(q r) m -> r q m", r=4)[r].bitcast(I32),
+                    in_=page_planes[b][r:P:QROWS, :].bitcast(I32),
                 )
 
         score_acc = {}
@@ -283,61 +285,103 @@ def tile_list_roast_profile_page_kernel(
         make_feature(0, 0)
         make_feature(0, 1)
         scatter(0, 0)
+        store_page(0, 0)
         make_feature(0, 2)
         scatter(0, 1)
+        store_page(0, 1)
         quantise_w1(0, 1, nc.scalar.copy)
-        round_page(0, 0)
+        page_bf = ring.tile([P, PACK, T2], BF16, name="page_bf", tag="wide", align_bytes=64)
+        first_x = ring.tile([P, J, PACK], BF16, name="first_x", tag="raw01", bufs=1, align_bytes=64)
+        for h in range(2):
+            x_bf[0, h] = first_x[:, halves[h], :]
+        nc.scalar.copy(page_bf[:, 0, :], page[0, 0][:])
         fetch(0, 0)
         make_feature(0, 3)
         scatter(0, 2)
+        store_page(0, 2)
         quantise_w1(1, 1, nc.scalar.copy)
-        round_page(0, 1)
+        nc.scalar.copy(page_bf[:, 1, :], page[0, 1][:])
         fetch(0, 1)
+        nc.scalar.copy(page_bf[:, 2, :], page[0, 2][:])
+        fetch(0, 2)
         make_feature(1, 0)
         scatter(0, 3)
-        round_page(0, 2)
-        fetch(0, 2)
-        round_page(0, 3)
+        store_page(0, 3)
+        nc.scalar.copy(page_bf[:, 3, :], page[0, 3][:])
         fetch(0, 3)
         def finish_page_chunk(c):
-            quantise_page(0, c, weave(page_bf[0], page_chunks[c], nc.scalar.copy))
+            woven = ring.tile([P, BANK, PACK], BF16, name="woven", tag="woven", bufs=4, align_bytes=64)
+            weave_into(woven[:], page_bf[:, :, page_chunks[c]], nc.scalar.copy)
+            quantise_page(0, c, woven[:])
             store_page_codes(0, c)
 
+        side_by_side = ring.tile([P, 2, T2], F32, name="side_by_side", tag="wide", align_bytes=64)
         scatter(1, 0)
+        store_page(1, 0)
         make_feature(1, 1)
         scatter(1, 1)
         for h in range(2):
             quantise_x(0, h)
         finish_page_chunk(0)
         finish_page_chunk(1)
+        store_page(1, 1)
+        last_rows = [
+            ring.tile([P, PACK, J], BF16, name="last_rows", tag="raw%d1" % h, bufs=1, align_bytes=64) for h in range(2)
+        ]
+        for h in range(2):
+            x_bf[1, h] = last_rows[h][:, 2 - h : 4 - h, :].rearrange("p r (j t) -> p (r j) t", t=PACK)
         fetch(1, 0)
+        nc.scalar.dma_start(out=side_by_side[:, 0, :], in_=page[1, 0][:])
         make_feature(1, 2)
         scatter(1, 2)
+        store_page(1, 2)
         finish_page_chunk(2)
-        round_page(1, 0)
-        fetch(1, 1)
+        nc.scalar.dma_start(out=side_by_side[:, 1, :], in_=page[1, 1][:])
         finish_page_chunk(3)
         store_page_planes(0)
+        fetch(1, 1)
         make_feature(1, 3)
         for h in range(2):
             score_pass(0, h)
-        round_page(1, 1)
-        round_page(1, 2)
+        last_page = ring.tile([P, T2, PACK], BF16, name="last_page", tag="wide", align_bytes=64)
+        weave_into(last_page[:, :, 0:2], side_by_side[:], nc.scalar.copy)
+        nc.scalar.copy(last_rows[0][:, 0, :], page[1, 2][:, page_halves[0]])
         fetch(1, 2)
+        nc.scalar.copy(last_rows[1][:, 0, :], page[1, 2][:, page_halves[1]])
         scatter(1, 3)
-        round_page(1, 3, slice(0, T2 // 2))
+        store_page(1, 3)
+        nc.scalar.copy(last_rows[0][:, 1, :], page[1, 3][:, page_halves[0]])
         fetch(1, 3, parts=2)
-        round_page(1, 3, slice(T2 // 2, T2))
-        for h in range(2):
-            quantise_x(1, h)
-            score_pass(1, h)
+        def weave_last(c):
+            weave_into(last_page[:, page_chunks[c], 2:4], last_rows[c // 2][:, 0:2, halves[c % 2]], nc.vector.tensor_copy)
+
+        def quantise_last(c):
+            quantise_page(1, c, last_page[:, page_chunks[c], :])
+
+        quantise_x(1, 0)
+        score_pass(1, 0)
+        weave_last(0)
+        quantise_last(0)
+        weave_last(1)
+        quantise_x(1, 1)
+        score_pass(1, 1)
+        quantise_last(1)
+        nc.vector.tensor_copy(last_rows[1][:, 1, :], page[1, 3][:, page_halves[1]])
+        for c in (2, 3):
+            weave_last(c)
+        for c in (2, 3):
+            quantise_last(c)
         for h in range(2):
             empty_scores(h)
-        for c in range(4):
-            quantise_page(1, c, weave(page_bf[1], page_chunks[c], nc.vector.tensor_copy))
-        for c in range(4):
-            store_page_codes(1, c)
-            if c < 3:
-                for k in range(3 * c, min(3 * c + 3, 8)):
-                    store_scores(k % 4, k // 4)
+        store_page_codes(1, 0)
+        for n in (0, 1):
+            store_scores(n, 0)
+        store_page_codes(1, 1)
+        for n in (2, 3):
+            store_scores(n, 0)
+        for n in (0, 1, 2):
+            store_scores(n, 1)
+        store_page_codes(1, 2)
+        store_scores(3, 1)
+        store_page_codes(1, 3)
         store_page_planes(1)

@@ -47,7 +47,7 @@ def tile_list_roast_profile_page_kernel(
 
         tab_planes = keep.tile([P, T], U8, name="tab_planes", tag="tab_planes", align_bytes=64)
         w4_planes = keep.tile([P, 2 * N], U8, name="w4_planes", align_bytes=64)
-        gain_cols = keep.tile([P, 2, PACK], F32, name="gain_cols")
+        gain_col = {}
         bias_cols = keep.tile([P, 2, PACK], F32, name="bias_cols")
         warm = keep.tile([P, 8], F32, name="warm")
         nc.vector.memset(tab_planes[:].bitcast(I32), 0)
@@ -95,13 +95,23 @@ def tile_list_roast_profile_page_kernel(
 
         nc.sync.dma_start(out=wgs_rows[:], in_=wgs)
         nc.sync.dma_start(pick[:], offs)
-        nc.sync.dma_start(out=gain_cols[:], in_=gain.rearrange("(b p t) -> p b t", b=2, t=PACK))
+        gain_rows = gain.rearrange("(b p t) -> p b t", b=2, t=PACK)
+
+        def load_gain(b, first, count):
+            cols = keep.tile([P, count], F32, name="gain%d%d" % (b, first))
+            nc.sync.dma_start(out=cols[:], in_=gain_rows[:, b, first : first + count])
+            for t in range(count):
+                gain_col[b, first + t] = cols[:, t : t + 1]
+
+        load_gain(0, 0, 4)
+        load_gain(1, 0, 2)
         load_w1(0, 0)
         load_table(0)
         load_w1(1, 0)
         load_table(1)
         nc.sync.dma_start(put[:], offs2)
         load_page(0, 0)
+        load_gain(1, 2, 2)
 
         ident = keep.tile([P, P], F32, name="ident")
         make_identity(nc, ident[:])
@@ -123,7 +133,7 @@ def tile_list_roast_profile_page_kernel(
                 for b in range(2):
                     nc.scalar.activation(
                         factor[b, t][:, halves[h]], dealt[:].rearrange("p c j -> p (c j)"), ACT.Copy,
-                        scale=gain_cols[:, b, t : t + 1],
+                        scale=gain_col[b, t],
                     )
 
         load_w1(0, 1)
@@ -141,7 +151,7 @@ def tile_list_roast_profile_page_kernel(
         w1_planes = {}
 
         def quantise_w1(a, b, copy):
-            if (a, b) == (1, 0):
+            if (a, b) == (0, 0):
                 grouped = keep.tile([P, GROUP * PACK], BF16, name="w1_grouped", tag="picked_planes", align_bytes=64)
             else:
                 grouped = ring.tile([P, GROUP * PACK], BF16, name="w1_grouped", tag="woven", bufs=4, align_bytes=64)
@@ -158,10 +168,10 @@ def tile_list_roast_profile_page_kernel(
         picked = [keep.tile([P, S], U32, name="picked%d" % a, align_bytes=64) for a in range(2)]
 
         quantise_w1(0, 0, nc.vector.tensor_copy)
-        nc.vector.tensor_copy(picked[0][:], tab[0][:].indirect(pick[:]))
-        quantise_w1(1, 0, nc.vector.tensor_copy)
         picked_planes = keep.tile([P, S], U8, name="picked_planes", tag="picked_planes", align_bytes=64)
         nc.vector.tensor_copy(picked_planes[:], tab_planes[:].indirect(pick[:]))
+        nc.vector.tensor_copy(picked[0][:], tab[0][:].indirect(pick[:]))
+        quantise_w1(1, 0, nc.vector.tensor_copy)
         for h in range(2):
             nc.vector.tensor_copy(picked[1][:, halves[h]], tab[1][:].indirect(pick[:, list_halves[h]]))
 

from contextlib import ExitStack

import concourse.mybir as mybir
from concourse.masks import make_identity

K, H, N, T, S, T2, J = 1024, 1024, 512, 4096, 1024, 2048, 1024
FLOPS = 2 * K * H * S + 2 * H * N * J

F32 = mybir.dt.float32
BF16 = mybir.dt.bfloat16
I32 = mybir.dt.int32
U32 = mybir.dt.uint32
U16 = mybir.dt.uint16
U8 = mybir.dt.uint8
FP8X4 = mybir.dt.float8_e4m3fn_x4
FP4X4 = mybir.dt.float4_e2m1fn_x4
ACT = mybir.ActivationFunctionType
MULT = mybir.AluOpType.mult

P = 128
PACK = 4
GROUP = P * PACK
QUADS = 4
QROWS = 32
BANK = 512
LIST_COLS = BANK // 16


def tile_list_roast_profile_page_kernel(
    tc, tab_words, tab_scales, offs, w1, gain, page0, wgs, offs2, offs3, b2, w4_words, w4_scales,
    out_0, out_1, out_2, out_3,
):
    nc = tc.nc
    with ExitStack() as ctx:
        lists = ctx.enter_context(tc.tile_pool(name="lists", bufs=1))
        keep = ctx.enter_context(tc.tile_pool(name="keep", bufs=1))
        ring = ctx.enter_context(tc.tile_pool(name="ring", bufs=2))
        psum = ctx.enter_context(tc.psum_pool(name="psum", bufs=4))

        pick = lists.tile([P, S // 16], U16, name="pick")
        put = lists.tile([P, S // 16], U16, name="put")
        read = lists.tile([P, J // 16], U16, name="read")

        slices = [(b, t) for b in range(2) for t in range(PACK)]
        halves = [slice(h * BANK, (h + 1) * BANK) for h in range(2)]
        list_halves = [slice(h * LIST_COLS, (h + 1) * LIST_COLS) for h in range(2)]

        tab_planes = keep.tile([P, T], U8, name="tab_planes", tag="tab_planes", align_bytes=64)
        w4_planes = keep.tile([P, 2 * N], U8, name="w4_planes", align_bytes=64)
        gain_col = {}
        bias_cols = keep.tile([P, 2, PACK], F32, name="bias_cols")
        warm = keep.tile([P, 8], F32, name="warm")
        nc.vector.memset(tab_planes[:].bitcast(I32), 0)
        nc.vector.memset(w4_planes[:].bitcast(I32), 0)
        nc.vector.memset(warm[:], 0.0)
        nc.scalar.activation(warm[:, 4:5], warm[:, 0:1], ACT.Tanh)

        for q in range(QUADS):
            nc.gpsimd.dma_start(
                out=tab_planes[QROWS * q : QROWS * q + 8, :].bitcast(I32),
                in_=tab_scales[:, 4 * q : 4 * q + 4, :].bitcast(I32),
            )

        def load_w4_planes():
            for q in range(QUADS):
                nc.sync.dma_start(
                    out=w4_planes[QROWS * q : QROWS * q + 4, :].bitcast(I32).rearrange("r (a c) -> r a c", a=2),
                    in_=w4_scales[:, 4 * q : 4 * q + 4, :].bitcast(I32).rearrange("a r c -> r a c"),
                )

        tab = [ring.tile([P, T], U32, name="tab%d" % a, tag="wide", align_bytes=64) for a in range(2)]
        wgs_rows = ring.tile([P, S], F32, name="wgs_rows", tag="woven", bufs=4, align_bytes=64)
        spread = [
            ring.tile([P, 4, PACK, P], F32, name="spread%d" % h, tag="raw%d1" % h, bufs=1, align_bytes=64) for h in range(2)
        ]
        w1_raw = {}
        for b in range(2):
            for a in range(2):
                w1_raw[a, b] = ring.tile([P, PACK, GROUP], F32, name="w1_raw%d%d" % (a, b), tag="raw%d%d" % (a, b), bufs=1, align_bytes=64)
        page = {bt: keep.tile([P, T2], F32, name="page%d%d" % bt) for bt in slices}
        w4_codes = [keep.tile([P, 2 * N], U8, name="w4_codes%d" % a, align_bytes=64) for a in range(2)]

        w1_rows = w1.rearrange("(a p j) (b c) -> a b p j c", a=2, j=PACK, b=2)
        page_rows = page0.rearrange("(b p t) m -> b t p m", b=2, t=PACK)
        out1_rows = out_1.rearrange("(b p t) m -> b t p m", b=2, t=PACK)

        def load_table(a):
            nc.sync.dma_start(out=tab[a][:].bitcast(I32), in_=tab_words[a].rearrange("p t i -> p (t i)").bitcast(I32))

        def load_w1(a, b):
            nc.sync.dma_start(out=w1_raw[a, b][:], in_=w1_rows[a, b])

        def load_page(b, t):
            nc.sync.dma_start(out=page[b, t][:], in_=page_rows[b, t])

        nc.sync.dma_start(out=wgs_rows[:], in_=wgs)
        nc.sync.dma_start(pick[:], offs)
        gain_rows = gain.rearrange("(b p t) -> p b t", b=2, t=PACK)

        def load_gain(b, first, count):
            cols = keep.tile([P, count], F32, name="gain%d%d" % (b, first))
            nc.sync.dma_start(out=cols[:], in_=gain_rows[:, b, first : first + count])
            for t in range(count):
                gain_col[b, first + t] = cols[:, t : t + 1]

        load_gain(0, 0, 4)
        load_gain(1, 0, 2)
        load_w1(0, 0)
        load_table(0)
        load_w1(1, 0)
        load_table(1)
        nc.sync.dma_start(put[:], offs2)
        load_page(0, 0)
        load_gain(1, 2, 2)

        ident = keep.tile([P, P], F32, name="ident")
        make_identity(nc, ident[:])
        for h in range(2):
            turned = psum.tile([P, 4, P], F32, name="turned", tag="bank0")
            for c in range(4):
                j0 = BANK * h + P * c
                nc.tensor.transpose(turned[:, c, :], wgs_rows[:, j0 : j0 + P], ident[:])
            (nc.scalar.copy, nc.vector.tensor_copy)[h](
                spread[h][:].rearrange("j c t (g q) -> j c t g q", g=QUADS),
                turned[:].rearrange("j c (q t) -> j c t q", t=PACK).unsqueeze(3).to_broadcast([P, 4, PACK, QUADS, QROWS]),
            )
        factor = {bt: keep.tile([P, S], F32, name="factor", tag="factor%d%d" % bt, align_bytes=64) for bt in slices}
        for t in range(PACK):
            for h in range(2):
                dealt = psum.tile([P, 4, P], F32, name="dealt", tag="bank0")
                for c in range(4):
                    nc.tensor.transpose(dealt[:, c, :], spread[h][:, c, t, :], ident[:])
                for b in range(2):
                    nc.scalar.activation(
                        factor[b, t][:, halves[h]], dealt[:].rearrange("p c j -> p (c j)"), ACT.Copy,
                        scale=gain_col[b, t],
                    )

        load_w1(0, 1)
        load_page(0, 1)
        nc.sync.dma_start(read[:], offs3)
        nc.sync.dma_start(out=bias_cols[:], in_=b2.rearrange("(b p t) -> p b t", b=2, t=PACK))
        load_w1(1, 1)
        for bt in slices[2:]:
            load_page(*bt)
        for a in range(2):
            nc.sync.dma_start(out=w4_codes[a][:].bitcast(I32), in_=w4_words[a].bitcast(I32))
        load_w4_planes()

        w1_codes = {}
        w1_planes = {}

        def quantise_w1(a, b, copy):
            if (a, b) == (0, 0):
                grouped = keep.tile([P, GROUP * PACK], BF16, name="w1_grouped", tag="picked_planes", align_bytes=64)
            else:
                grouped = ring.tile([P, GROUP * PACK], BF16, name="w1_grouped", tag="woven", bufs=4, align_bytes=64)
            copy(
                grouped[:].rearrange("p (t m j) -> p m j t", t=PACK, j=PACK),
                w1_raw[a, b][:].rearrange("p j (m t) -> p m j t", t=PACK),
            )
            w1_codes[a, b] = keep.tile(
                [P, GROUP], U32, name="w1_codes", tag="factor0%d" % (a + 1) if b else "w1_codes%d" % a, align_bytes=64
            )
            w1_planes[a, b] = keep.tile([P, GROUP], U8, name="w1_planes%d%d" % (a, b), align_bytes=64)
            nc.vector.quantize_mx(out=w1_codes[a, b][:].bitcast(FP8X4), scales=w1_planes[a, b][:], in_=grouped[:])

        picked = [keep.tile([P, S], U32, name="picked%d" % a, align_bytes=64) for a in range(2)]

        quantise_w1(0, 0, nc.vector.tensor_copy)
        picked_planes = keep.tile([P, S], U8, name="picked_planes", tag="picked_planes", align_bytes=64)
        nc.vector.tensor_copy(picked_planes[:], tab_planes[:].indirect(pick[:]))
        nc.vector.tensor_copy(picked[0][:], tab[0][:].indirect(pick[:]))
        quantise_w1(1, 0, nc.vector.tensor_copy)
        for h in range(2):
            nc.vector.tensor_copy(picked[1][:, halves[h]], tab[1][:].indirect(pick[:, list_halves[h]]))

        feature = {}

        def make_feature(b, t):
            feature[b, t] = ring.tile([P, S], F32, name="feature", tag="feature")
            cols = slice(P * t, P * (t + 1))
            for h in range(2):
                acc = psum.tile([P, BANK], F32, name="acc", tag="bank1")
                for a in range(2):
                    nc.tensor.matmul_mx(
                        out=acc[:],
                        lhsT=w1_codes[a, b][:, cols].bitcast(FP8X4),
                        lhsT_scale=w1_planes[a, b][:, cols],
                        rhs=picked[a][:, halves[h]].bitcast(FP8X4),
                        rhs_scale=picked_planes[4 * a :, halves[h]],
                        start=(a == 0),
                        stop=(a == 1),
                    )
                nc.scalar.activation(feature[b, t][:, halves[h]], acc[:], ACT.Tanh)

        def scatter(b, t):
            if (b, t) == slices[0]:
                for h in range(2):
                    nc.vector.tensor_tensor(
                        page[b, t][:].indirect(put[:, list_halves[h]]),
                        feature[b, t][:, halves[h]], factor[b, t][:, halves[h]], MULT,
                    )
            else:
                nc.vector.tensor_tensor(page[b, t][:].indirect(put[:]), feature[b, t][:], factor[b, t][:], MULT)

        def store_page(b, t):
            nc.sync.dma_start(out=out1_rows[b, t], in_=page[b, t][:])

        page_halves = [slice(h * T2 // 2, (h + 1) * T2 // 2) for h in range(2)]
        x_bf = {}
        x_rows = {}

        def fetch(b, t, parts=1):
            fetched = ring.tile([P, J], F32, name="fetched", tag="raw%d0" % (t % 2), bufs=1, align_bytes=64)
            for part in range(parts):
                cols = slice(part * J // parts, (part + 1) * J // parts)
                entries = slice(cols.start // 16, cols.stop // 16)
                nc.vector.tensor_copy(fetched[:, cols], page[b, t][:].indirect(read[:, entries]))
            bias = bias_cols[:, b, t : t + 1]
            if t == 0:
                x_rows[b] = keep.tile([P, PACK - 1, J], BF16, name="x_rows", tag="factor00", align_bytes=64)
            if t < PACK - 1:
                nc.scalar.activation(x_rows[b][:, t, :], fetched[:], ACT.Identity, bias=bias)
            for h in range(2):
                if t == PACK - 2:
                    weave_into(x_bf[b, h][:, :, : PACK - 1], x_rows[b][:, :, halves[h]], nc.scalar.copy)
                if t == PACK - 1:
                    nc.scalar.activation(x_bf[b, h][:, :, t], fetched[:, halves[h]], ACT.Identity, bias=bias)

        def weave_into(woven, rows, copy):
            copy(woven.rearrange("p (c i) t -> p c t i", i=4), rows.rearrange("p t (c i) -> p c t i", i=4))

        x_codes = [
            keep.tile([P, J], U32, name="x_codes", tag=tag, align_bytes=64) for tag in ("x_codes", "tab_planes")
        ]
        x_planes = [keep.tile([P, J], U8, name="x_planes%d" % b, align_bytes=64) for b in range(2)]
        page_codes = [keep.tile([P, T2], U32, name="page_codes%d" % b, align_bytes=64) for b in range(2)]
        page_planes = [keep.tile([P, T2], U8, name="page_planes%d" % b, align_bytes=64) for b in range(2)]

        def quantise_x(b, h):
            nc.vector.quantize_mx(
                out=x_codes[b][:, halves[h]].bitcast(FP8X4),
                scales=x_planes[b][:, halves[h]],
                in_=x_bf[b, h].rearrange("p j t -> p (j t)"),
            )

        def quantise_page(b, c, woven):
            cols = slice(c * BANK, (c + 1) * BANK)
            nc.vector.quantize_mx(out=page_codes[b][:, cols].bitcast(FP8X4), scales=page_planes[b][:, cols], in_=woven.rearrange("p m t -> p (m t)"))

        def store_page_codes(b, c):
            cols = slice(c * BANK, (c + 1) * BANK)
            nc.sync.dma_start(
                out=out_2[b].rearrange("p m t -> p (m t)").bitcast(I32)[:, cols],
                in_=page_codes[b][:, cols].bitcast(I32),
            )

        def store_page_planes(b):
            for r in range(4):
                nc.sync.dma_start(
                    out=out_3[b].rearrange("(q r) m -> r q m", r=4)[r].bitcast(I32),
                    in_=page_planes[b][r:P:QROWS, :].bitcast(I32),
                )

        score_acc = {}

        def score_pass(b, h):
            for n in range(N // P):
                if b == 0:
                    score_acc[n, h] = psum.tile([P, BANK], F32, name="score_acc", tag="bank%d" % h)
                nc.tensor.matmul_mx(
                    out=score_acc[n, h][:],
                    lhsT=w4_codes[b][:, 2 * P * n : 2 * P * (n + 1)].bitcast(FP4X4),
                    lhsT_scale=w4_planes[:, N * b + P * n : N * b + P * (n + 1)],
                    rhs=x_codes[b][:, halves[h]].bitcast(FP8X4),
                    rhs_scale=x_planes[b][:, halves[h]],
                    start=(b == 0),
                    stop=(b == 1),
                )

        score = {}

        def empty_scores(h):
            for n in range(N // P):
                if h == 0:
                    score[n] = keep.tile([P, J], F32, name="score", tag="factor1%d" % n, align_bytes=64)
                nc.scalar.copy(score[n][:, halves[h]], score_acc[n, h][:])

        def store_scores(n, h):
            nc.sync.dma_start(out=out_0[P * n : P * (n + 1), halves[h]], in_=score[n][:, halves[h]])

        page_chunks = [slice(c * BANK, (c + 1) * BANK) for c in range(T2 // BANK)]

        make_feature(0, 0)
        make_feature(0, 1)
        scatter(0, 0)
        store_page(0, 0)
        make_feature(0, 2)
        scatter(0, 1)
        store_page(0, 1)
        quantise_w1(0, 1, nc.scalar.copy)
        page_bf = ring.tile([P, PACK, T2], BF16, name="page_bf", tag="wide", align_bytes=64)
        first_x = ring.tile([P, J, PACK], BF16, name="first_x", tag="raw01", bufs=1, align_bytes=64)
        for h in range(2):
            x_bf[0, h] = first_x[:, halves[h], :]
        nc.scalar.copy(page_bf[:, 0, :], page[0, 0][:])
        fetch(0, 0)
        make_feature(0, 3)
        scatter(0, 2)
        store_page(0, 2)
        quantise_w1(1, 1, nc.scalar.copy)
        nc.scalar.copy(page_bf[:, 1, :], page[0, 1][:])
        fetch(0, 1)
        nc.scalar.copy(page_bf[:, 2, :], page[0, 2][:])
        fetch(0, 2)
        make_feature(1, 0)
        scatter(0, 3)
        store_page(0, 3)
        nc.scalar.copy(page_bf[:, 3, :], page[0, 3][:])
        fetch(0, 3)
        def finish_page_chunk(c):
            woven = ring.tile([P, BANK, PACK], BF16, name="woven", tag="woven", bufs=4, align_bytes=64)
            weave_into(woven[:], page_bf[:, :, page_chunks[c]], nc.scalar.copy)
            quantise_page(0, c, woven[:])
            store_page_codes(0, c)

        side_by_side = ring.tile([P, 2, T2], F32, name="side_by_side", tag="wide", align_bytes=64)
        scatter(1, 0)
        store_page(1, 0)
        make_feature(1, 1)
        scatter(1, 1)
        for h in range(2):
            quantise_x(0, h)
        finish_page_chunk(0)
        finish_page_chunk(1)
        store_page(1, 1)
        last_rows = [
            ring.tile([P, PACK, J], BF16, name="last_rows", tag="raw%d1" % h, bufs=1, align_bytes=64) for h in range(2)
        ]
        for h in range(2):
            x_bf[1, h] = last_rows[h][:, 2 - h : 4 - h, :].rearrange("p r (j t) -> p (r j) t", t=PACK)
        fetch(1, 0)
        nc.scalar.dma_start(out=side_by_side[:, 0, :], in_=page[1, 0][:])
        make_feature(1, 2)
        scatter(1, 2)
        store_page(1, 2)
        finish_page_chunk(2)
        nc.scalar.dma_start(out=side_by_side[:, 1, :], in_=page[1, 1][:])
        finish_page_chunk(3)
        store_page_planes(0)
        fetch(1, 1)
        make_feature(1, 3)
        for h in range(2):
            score_pass(0, h)
        last_page = ring.tile([P, T2, PACK], BF16, name="last_page", tag="wide", align_bytes=64)
        weave_into(last_page[:, :, 0:2], side_by_side[:], nc.scalar.copy)
        nc.scalar.copy(last_rows[0][:, 0, :], page[1, 2][:, page_halves[0]])
        fetch(1, 2)
        nc.scalar.copy(last_rows[1][:, 0, :], page[1, 2][:, page_halves[1]])
        scatter(1, 3)
        store_page(1, 3)
        nc.scalar.copy(last_rows[0][:, 1, :], page[1, 3][:, page_halves[0]])
        fetch(1, 3, parts=2)
        def weave_last(c):
            weave_into(last_page[:, page_chunks[c], 2:4], last_rows[c // 2][:, 0:2, halves[c % 2]], nc.vector.tensor_copy)

        def quantise_last(c):
            quantise_page(1, c, last_page[:, page_chunks[c], :])

        quantise_x(1, 0)
        score_pass(1, 0)
        weave_last(0)
        quantise_last(0)
        weave_last(1)
        quantise_x(1, 1)
        score_pass(1, 1)
        quantise_last(1)
        nc.vector.tensor_copy(last_rows[1][:, 1, :], page[1, 3][:, page_halves[1]])
        for c in (2, 3):
            weave_last(c)
        for c in (2, 3):
            quantise_last(c)
        for h in range(2):
            empty_scores(h)
        store_page_codes(1, 0)
        for n in (0, 1):
            store_scores(n, 0)
        store_page_codes(1, 1)
        for n in (2, 3):
            store_scores(n, 0)
        for n in (0, 1, 2):
            store_scores(n, 1)
        store_page_codes(1, 2)
        store_scores(3, 1)
        store_page_codes(1, 3)
        store_page_planes(1)
